import numpy as np
import ml_dtypes


def mxq(x, axis, fmt="e4m3"):
    dtype, down = {"e4m3": (ml_dtypes.float8_e4m3fn, 7), "e5m2": (ml_dtypes.float8_e5m2, 14)}[fmt]
    v = np.moveaxis(np.asarray(x, np.float32).astype(ml_dtypes.bfloat16).astype(np.float64), axis, -1)
    blocks = v.reshape(v.shape[:-1] + (-1, 32))
    amax = np.abs(blocks).max(-1, keepdims=True)
    byte = np.maximum(np.where(amax > 0, np.frexp(amax)[1] - 1 + 127, 0) - down, 1)
    scale = np.exp2(byte - 127.0)
    codes = (blocks / scale).astype(np.float32).astype(dtype).astype(np.float64)
    return np.moveaxis((codes * scale).reshape(v.shape), -1, axis)


WIDE = False


def mx_kscale(k):
    if not WIDE:
        return np.ones(k)
    levels = np.array([10, -10, 5, -5, 0])
    if k % 512:
        return np.exp2(np.random.permutation(np.resize(levels, k // 32))).repeat(32)
    a = np.empty((k // 512, 16))
    for p in range(k // 512):
        a[p, :8] = np.random.permutation(np.resize(levels, 8))
        for g in range(8):
            far = levels[np.abs(levels - a[p, g]) >= 10]
            a[p, g + 8] = far[np.random.randint(len(far))]
    return np.exp2(a.ravel()).repeat(32)


def f64(x):
    return np.asarray(x).astype(np.float64)


def striped(idx):
    return np.tile(np.asarray(idx).reshape(-1, 16).T, (8, 1)).astype(np.uint16)


def unstriped(offs):
    return offs[:16].T.reshape(-1).astype(np.int64)


E2M1 = np.array([0.0, 0.5, 1.0, 1.5, 2.0, 3.0, 4.0, 6.0, -0.0, -0.5, -1.0, -1.5, -2.0, -3.0, -4.0, -6.0])


def pack_weight(w, fmt):
    k, n = w.shape
    w = f64(np.asarray(w, np.float32).astype(ml_dtypes.bfloat16)).reshape(k // 32, 32, n)
    amax = np.abs(w).max(1)
    if fmt == "e4m3":
        byte = np.frexp(amax)[1] - 1 + 127 - 7
    else:
        mant, ex = np.frexp(amax / 6.0)
        byte = np.where(mant > 0.5, ex, ex - 1) + 127
    byte = np.clip(np.where(amax > 0, byte, 1), 1, 254)
    scaled = (w * np.exp2(127.0 - byte)[:, None, :]).reshape(k, n).astype(np.float32)
    by_word = np.ascontiguousarray(scaled.reshape(k // 512, 128, 4, n).transpose(0, 1, 3, 2))
    if fmt == "e4m3":
        words = by_word.astype(ml_dtypes.float8_e4m3fn).view(np.uint8)
    else:
        c = by_word.astype(ml_dtypes.float4_e2m1fn).view(np.uint8) & 0xF
        words = (c[..., 0::2] | (c[..., 1::2] << 4)).reshape(k // 512, 128, 2 * n)
    return np.ascontiguousarray(words), np.ascontiguousarray(byte.astype(np.uint8).reshape(k // 512, 16, n))


def unpack_weight(words, scales, fmt):
    g, _, n = scales.shape
    words = np.ascontiguousarray(words).reshape(g, 128, n, -1)
    if fmt == "e4m3":
        vals = words.view(ml_dtypes.float8_e4m3fn).astype(np.float64)
    else:
        nib = np.empty((g, 128, n, 4), np.uint8)
        nib[..., 0::2] = words & 0xF
        nib[..., 1::2] = words >> 4
        vals = E2M1[nib]
    vals = vals * np.repeat(np.exp2(scales.astype(np.float64) - 127.0), 8, axis=1)[..., None]
    return vals.transpose(0, 1, 3, 2).reshape(g * 512, n)


def bf(x):
    return np.asarray(x, np.float32).astype(ml_dtypes.bfloat16)


def planes(Y):
    r, m = Y.shape
    b = f64(bf(Y)).reshape(r // 32, 32, m)
    amax = np.abs(b).max(1)
    byte = np.clip(np.where(amax > 0, np.frexp(amax)[1] - 1 + 127 - 7, 1), 1, 254)
    codes = (b * np.exp2(127.0 - byte)[:, None, :]).reshape(r, m).astype(np.float32).astype(ml_dtypes.float8_e4m3fn).view(np.uint8)
    words = codes.reshape(r // 512, 128, 4, m).transpose(0, 1, 3, 2)
    return np.ascontiguousarray(words), np.ascontiguousarray(byte.astype(np.uint8).reshape(r // 512, 16, m))


D, T, I, Q, E, G = 512, 2048, 512, 256, 512, 64


def setup_inputs():
    n = np.random.standard_normal
    idx = np.random.permutation(T)[:I]
    fd = mx_kscale(D)
    fi = mx_kscale(I)
    ti = np.ones(T)
    ti[idx] = fi
    keysp = pack_weight(n((D, T)) / fd[:, None], "e2m1")
    return {
        "query": (n((D, Q)) * 0.7 / np.sqrt(D) * fd[:, None]).astype(np.float32),
        "query2": (n((D, Q)) * 0.7 / np.sqrt(D) * fd[:, None]).astype(np.float32),
        "keys_words": keysp[0],
        "keys_scales": keysp[1],
        "xmark": np.tile(np.random.uniform(-1.0, 1.0, T), (128, 1)).astype(np.float32),
        "ymark": np.tile(np.random.uniform(-1.0, 1.0, T), (128, 1)).astype(np.float32),
        "lam": (np.random.uniform(0.5, 1.2, (Q, 1))).astype(np.float32),
        "os": (np.random.uniform(4.0, 16.0, (1, I)) * fi).astype(np.float32),
        "vals": (n((E, T)) / ti).astype(np.float32),
        "memq": (np.random.uniform(0.3, 1.0, (1, Q))).astype(np.float32),
        "offs": striped(idx),
    }


def reference(query, query2, keys_words, keys_scales, xmark, ymark, lam, os, vals, memq, offs):
    idx = unstriped(offs)
    keysu = unpack_weight(keys_words, keys_scales, "e2m1")
    queryq = mxq(f64(query), 0, "e4m3")
    keysidxg = keysu[:, idx]
    a = queryq.T @ keysidxg
    query2q = mxq(f64(query2), 0, "e4m3")
    b = query2q.T @ keysidxg
    dx = a - f64(xmark)[:1][:, idx]
    dy = b - f64(ymark)[:1][:, idx]
    s = (np.square(dx) + np.square(dy)) * f64(lam) * (-1.0)
    p = np.exp(s)
    pg = p.reshape(Q, G, I // G).sum(axis=2)
    rt0 = np.sqrt(pg)
    k0 = rt0 / np.sum(rt0, axis=1, keepdims=True) / np.square(pg)
    kr = np.repeat(k0, I // G, axis=1)
    w = np.square(p) * kr
    wo1 = w * f64(os)
    wt1 = wo1.T
    vt1 = f64(vals)[:, idx].T
    vt1q = mxq(vt1, 0, "e4m3")
    wt1q = mxq(wt1, 0, "e4m3")
    o = vt1q.T @ wt1q
    o1 = np.pad(o, ((0, 0), (1, 0)))[:, :Q]
    y = o - o1 * f64(memq)
    words, scales = planes(y)
    return y, words, scales

@@ -1,0 +1,261 @@
+from contextlib import ExitStack
+
+import concourse.mybir as mybir
+from concourse.masks import make_identity
+
+D, T, I, Q, E, G = 512, 2048, 512, 256, 512, 64
+FLOPS = 2 * D * I * Q * 2 + 2 * I * E * Q
+
+F32 = mybir.dt.float32
+BF16 = mybir.dt.bfloat16
+I32 = mybir.dt.int32
+U32 = mybir.dt.uint32
+U16 = mybir.dt.uint16
+U8 = mybir.dt.uint8
+FP8X4 = mybir.dt.float8_e4m3fn_x4
+FP4X4 = mybir.dt.float4_e2m1fn_x4
+ACT = mybir.ActivationFunctionType
+ALU = mybir.AluOpType
+
+P = 128
+TINY = 2.0 ** -80
+
+
+def tile_attend_maplace_pagewinners_rowchanges_pl_kernel(
+    tc, query, query2, keys_words, keys_scales, xmark, ymark, lam, slot_scale, vals, memq, offs, out_0, out_1, out_2
+):
+    nc = tc.nc
+    with ExitStack() as ctx:
+        sb = ctx.enter_context(tc.tile_pool(name="sb", bufs=1))
+        ps = ctx.enter_context(tc.psum_pool(name="ps", bufs=1))
+
+        def bank(b, name):
+            return ps.tile([P, 512], F32, name=name, tag="bank%d" % b)
+
+        def tile(shape, dtype, name, tag=None):
+            return sb.tile(shape, dtype, name=name, tag=tag or name, align_bytes=64)
+
+        offsets = sb.tile([P, I // 16], U16, name="offsets")
+        nc.sync.dma_start(offsets[:], offs)
+
+        mark_pools = [tile([P, T], F32, "mark_pool%d" % c) for c in range(2)]
+        for c, src in enumerate((xmark, ymark)):
+            nc.sync.dma_start(mark_pools[c][P - 1 : P, :], src[0:1, :])
+        nc.vector.memset(mark_pools[0][0 : P - 1, :].bitcast(I32), 0)
+        nc.vector.memset(mark_pools[1][0 : P - 1, :].bitcast(I32), 0)
+        q_raw = [tile([P, 4, Q], F32, "q_raw%d" % c) for c in range(2)]
+        nc.sync.dma_start(q_raw[0][:], query.rearrange("(p j) w -> p j w", j=4))
+        nc.sync.dma_start(q_raw[1][:], query2.rearrange("(p j) w -> p j w", j=4))
+        kw_pool = tile([P, T], U16, "kw_pool")
+        nc.sync.dma_start(kw_pool[:].bitcast(I32), keys_words[0].bitcast(I32))
+        ks_pool = tile([P, T], U8, "ks_pool")
+        for quad in range(4):
+            rows = keys_scales[0, 4 * quad : 4 * quad + 4, :].bitcast(I32)
+            nc.sync.dma_start(
+                ks_pool[32 * quad : 32 * quad + 32, :].bitcast(I32), rows.unsqueeze(0).to_broadcast([8, 4, T // 4])
+            )
+        vals_dealt = vals.rearrange("(p t) c -> p t c", t=4)
+        v_pools = [tile([P, T], F32, "v_pool%d" % t) for t in range(4)]
+        nc.sync.dma_start(v_pools[0][:], vals_dealt[:, 0, :])
+        lam_c = tile([P, 2], F32, "lam_c")
+        mem_c = tile([P, 2], F32, "mem_c")
+        os_c = tile([P, 4], F32, "os_c")
+        with nc.allow_non_contiguous_dma(reason="one value a partition"):
+            nc.sync.dma_start(lam_c[:], lam.rearrange("(c p) o -> p (c o)", p=P))
+            nc.sync.dma_start(mem_c[:], memq.rearrange("o (c p) -> p (o c)", p=P))
+        nc.sync.dma_start(os_c[:], slot_scale.rearrange("o (p r) -> p (o r)", r=4))
+        for t in range(1, 4):
+            nc.sync.dma_start(v_pools[t][:], vals_dealt[:, t, :])
+
+        ident = tile([P, P], F32, "ident")
+        make_identity(nc, ident[:])
+        y_prev = tile([P, 4, Q], F32, "y_prev")
+        nc.gpsimd.memset(y_prev[:, :, 0:1], 0.0)
+
+        q_codes = tile([P, 2 * Q], U32, "q_codes")
+        q_scales = tile([P, 2 * Q], U8, "q_scales")
+        q_bf = [tile([P, Q, 4], BF16, "q_bf%d" % c) for c in range(2)]
+        for c in range(2):
+            nc.scalar.copy(
+                q_bf[c][:].rearrange("p (c i) t -> p c t i", i=4), q_raw[c][:].rearrange("p t (c i) -> p c t i", i=4)
+            )
+
+        marks = []
+        for c in range(2):
+            picked = tile([P, I], F32, "mark_picked%d" % c)
+            nc.vector.tensor_copy(picked[:], mark_pools[c][:].indirect(offsets[:]))
+            turned = bank(6 + c, "marks_turned%d" % c)
+            for j in range(4):
+                nc.tensor.transpose(turned[:, P * j : P * (j + 1)], picked[:, P * j : P * (j + 1)], ident[:])
+            mk = tile([P, 4], F32, "marks%d" % c)
+            nc.scalar.copy(mk[:], turned[:, P - 1 :: P])
+            marks.append(mk)
+
+        scores = []
+        for h in range(2):
+            half = offsets[:, 16 * h : 16 * h + 16]
+            kw = tile([P, 256], U16, "kw%d" % h, tag="q_bf0" if h else None)
+            ks = tile([P, 256], U8, "ks%d" % h, tag="q_bf1" if h else None)
+            nc.vector.tensor_copy(kw[:], kw_pool[:].indirect(half))
+            nc.vector.tensor_copy(ks[:], ks_pool[:].indirect(half))
+            if h == 0:
+                for c in range(2):
+                    nc.vector.quantize_mx(
+                        out=q_codes[:, Q * c : Q * (c + 1)].bitcast(FP8X4),
+                        scales=q_scales[:, Q * c : Q * (c + 1)],
+                        in_=q_bf[c][:].rearrange("p q t -> p (q t)"),
+                    )
+            for jj in range(2):
+                cols = slice(P * jj, P * (jj + 1))
+                score = bank(2 * h + jj, "score%d%d" % (h, jj))
+                nc.tensor.matmul_mx(
+                    out=score[:], lhsT=kw[:, cols].bitcast(FP4X4), lhsT_scale=ks[:, cols],
+                    rhs=q_codes[:].bitcast(FP8X4), rhs_scale=q_scales[:], start=True, stop=True,
+                )
+                scores.append(score)
+
+        neg_lam = tile([P, 2], F32, "neg_lam")
+        nc.gpsimd.tensor_scalar(neg_lam[:], lam_c[:], -1.0, 0.0, ALU.mult, ALU.add)
+
+        dist = [bank(4 + qt, "dist%d" % qt) for qt in range(2)]
+        for j in range(4):
+            score = scores[j]
+            sq = tile([P, 2, Q], F32, "sq%d" % j)
+            for c in range(2):
+                nc.scalar.activation(
+                    sq[:, c, :], score[:, Q * c : Q * (c + 1)], ACT.Square, bias=marks[c][:, j : j + 1], scale=-1.0
+                )
+            for qt in range(2):
+                for c in range(2):
+                    nc.tensor.matmul(
+                        dist[qt][:, P * j : P * (j + 1)], sq[:, c, P * qt : P * (qt + 1)], ident[:],
+                        start=(c == 0), stop=(c == 1), is_transpose=True,
+                    )
+
+        p = tile([P, 8, 2, G], F32, "p")
+        z = tile([P, 2], F32, "z")
+        for qt in range(2):
+            nc.scalar.activation(
+                p[:, :, qt, :], dist[qt][:].rearrange("p (g j) -> p j g", j=8), ACT.Exp,
+                scale=neg_lam[:, qt : qt + 1], accum_out=z[:, qt : qt + 1],
+            )
+        rz = tile([P, 2], F32, "rz")
+        rz_root = tile([P, 2], F32, "rz_root")
+        nc.scalar.activation(rz_root[:], z[:], ACT.Abs_reciprocal_sqrt)
+        nc.scalar.activation(rz[:], rz_root[:], ACT.Square)
+
+        v_mx = []
+        for t in range(4):
+            v_picked = tile([P, I], BF16, "v_picked%d" % t)
+            nc.vector.tensor_copy(v_picked[:], v_pools[t][:].indirect(offsets[:]))
+            words = v_picked[:].bitcast(F32)
+            v_turned = bank(6 + t % 2, "v_turned%d" % t)
+            for u in range(2):
+                nc.tensor.transpose(v_turned[:, P * u : P * (u + 1)], words[:, u::2], ident[:])
+            v_bf = tile([P, I], BF16, "v_bf%d" % t, tag=("marks1", "neg_lam", None, None)[t])
+            nc.scalar.copy(
+                v_bf[:].bitcast(F32).rearrange("p (e u) -> p e u", u=2),
+                v_turned[:, 0 : 2 * P].rearrange("p (u e) -> p e u", u=2),
+            )
+            v_codes = tile([P, P], U32, "v_codes%d" % t)
+            v_scales = tile([P, P], U8, "v_scales%d" % t)
+            nc.vector.quantize_mx(out=v_codes[:].bitcast(FP8X4), scales=v_scales[:], in_=v_bf[:])
+            v_mx.append((v_codes, v_scales))
+
+        pg_turned = bank(0, "pg_turned")
+        for j in range(8):
+            nc.tensor.matmul(
+                pg_turned[:, 0:P], p[:, j].rearrange("p t g -> p (t g)"), ident[:],
+                start=(j == 0), stop=(j == 7), is_transpose=True,
+            )
+        pg_t = tile([P, P], F32, "pg_t", tag="v_pool1")
+        nc.vector.tensor_copy(pg_t[:], pg_turned[:, 0:P])
+        pg = bank(1, "pg")
+        nc.tensor.transpose(pg[:, 0:P], pg_t[:], ident[:])
+
+        inv_rt = tile([P, 2, G], F32, "inv_rt")
+        inv_pg = tile([P, 2, G], F32, "inv_pg")
+        rt = tile([P, 2, G], F32, "rt", tag="v_pool2")
+        rt_sum = tile([P, 2], F32, "rt_sum")
+        for qt in range(2):
+            nc.scalar.activation(
+                inv_rt[:, qt, :], pg[:, G * qt : G * (qt + 1)], ACT.Abs_reciprocal_sqrt, bias=TINY, scale=rz[:, qt : qt + 1]
+            )
+        nc.scalar.activation(inv_pg[:], inv_rt[:], ACT.Square)
+        inv_sum = tile([P, 2], F32, "inv_sum")
+        k_twice = tile([P, 2, G, 2], F32, "k_twice")
+        for qt in range(2):
+            nc.vector.scalar_tensor_tensor(
+                rt[:, qt, :], pg[:, G * qt : G * (qt + 1)], rz[:, qt : qt + 1], inv_rt[:, qt, :], ALU.mult, ALU.mult,
+                accum_out=rt_sum[:, qt : qt + 1],
+            )
+        nc.vector.reciprocal(inv_sum[:], rt_sum[:])
+        p_dealt = p[:].rearrange("p (e r) t g -> p t r g e", r=4)
+        w_mx = []
+        for qt in range(2):
+            k_turned = bank(4 + qt, "k_turned%d" % qt)
+            nc.vector.scalar_tensor_tensor(
+                k_twice[:, qt], inv_pg[:, qt, :].unsqueeze(2).to_broadcast([P, G, 2]), inv_sum[:, qt : qt + 1],
+                inv_rt[:, qt, :].unsqueeze(2).to_broadcast([P, G, 2]), ALU.mult, ALU.mult,
+            )
+            nc.tensor.transpose(k_turned[:, 0:P], k_twice[:, qt].rearrange("p g e -> p (g e)"), ident[:])
+            p2 = tile([P, 4, G, 2], F32, "p2_%d" % qt)
+            nc.scalar.activation(p2[:], p_dealt[:, qt], ACT.Square, scale=rz[:, qt : qt + 1])
+            p2_os = tile([P, 4, P], F32, "p2_os%d" % qt)
+            p2_turned = bank(2 + qt, "p2_turned%d" % qt)
+            for r in range(4):
+                nc.tensor.transpose(p2_turned[:, P * r : P * (r + 1)], p2[:, r].rearrange("p g e -> p (g e)"), ident[:])
+            for r in range(4):
+                nc.scalar.activation(p2_os[:, r, :], p2_turned[:, P * r : P * (r + 1)], ACT.Copy, scale=os_c[:, r : r + 1])
+            w_bf = tile([P, P, 4], BF16, "w_bf%d" % qt, tag="p2_os0" if qt else "v_pool3")
+            nc.vector.tensor_tensor(
+                w_bf[:].rearrange("p (c i) r -> p c r i", i=4),
+                p2_os[:].rearrange("p r (c i) -> p c r i", i=4),
+                k_turned[:, 0:P].rearrange("p (c i) -> p c i", i=4).unsqueeze(2).to_broadcast([P, P // 4, 4, 4]),
+                ALU.mult,
+            )
+            w_codes = tile([P, P], U32, "w_codes%d" % qt)
+            w_scales = tile([P, P], U8, "w_scales%d" % qt)
+            nc.vector.quantize_mx(out=w_codes[:].bitcast(FP8X4), scales=w_scales[:], in_=w_bf[:].rearrange("p q r -> p (q r)"))
+            w_mx.append((w_codes, w_scales))
+
+        mem_turned = bank(0, "mem_turned")
+        for qt in range(2):
+            nc.tensor.transpose(mem_turned[:, P * qt : P * (qt + 1)], mem_c[:, qt : qt + 1].to_broadcast([P, P]), ident[:])
+        mem_row = tile([P, Q], F32, "mem_row")
+        nc.scalar.copy(mem_row[:], mem_turned[:, 0:Q])
+
+        out_dealt = out_0.rearrange("(p t) q -> p t q", t=4)
+        y_codes = tile([P, Q], U32, "y_codes")
+        y_scales = tile([P, Q], U8, "y_scales")
+        words_out = out_1[0].rearrange("p c r -> p (c r)").bitcast(I32)
+        for qt in range(2):
+            w_codes, w_scales = w_mx[qt]
+            cols = slice(P * qt, P * (qt + 1))
+            o = bank(qt, "o%d" % qt)
+            for t in range(4):
+                v_codes, v_scales = v_mx[t]
+                nc.tensor.matmul_mx(
+                    out=o[:, P * t : P * (t + 1)], lhsT=v_codes[:].bitcast(FP8X4), lhsT_scale=v_scales[:],
+                    rhs=w_codes[:].bitcast(FP8X4), rhs_scale=w_scales[:], start=True, stop=True,
+                )
+            o3 = o[:].rearrange("p (t q) -> p t q", t=4)
+            n = P - qt
+            nxt = slice(P * qt + 1, P * qt + 1 + n)
+            nc.vector.tensor_tensor(
+                y_prev[:, :, nxt], o3[:, :, 0:n], mem_row[:, nxt].unsqueeze(1).to_broadcast([P, 4, n]), ALU.mult
+            )
+            y = tile([P, 4, P], F32, "y%d" % qt)
+            nc.vector.tensor_tensor(y[:], o3, y_prev[:, :, cols], ALU.subtract)
+            nc.sync.dma_start(out_dealt[:, :, cols], y[:])
+            y_bf = tile([P, P, 4], BF16, "y_bf%d" % qt)
+            nc.scalar.copy(y_bf[:].rearrange("p (c i) t -> p c t i", i=4), y[:].rearrange("p t (c i) -> p c t i", i=4))
+            nc.vector.quantize_mx(
+                out=y_codes[:, cols].bitcast(FP8X4), scales=y_scales[:, cols], in_=y_bf[:].rearrange("p q t -> p (q t)")
+            )
+            nc.sync.dma_start(words_out[:, cols], y_codes[:, cols].bitcast(I32))
+        for quad in range(4):
+            queue = nc.scalar if quad % 2 else nc.sync
+            queue.dma_start(
+                out_2[0, 4 * quad : 4 * quad + 4, :].bitcast(I32), y_scales[32 * quad : 32 * quad + 4, :].bitcast(I32)
+            )

@@ -39,143 +39,153 @@ def tile_attend_maplace_pagewinners_rowchanges_pl_kernel(
         nc.sync.dma_start(offsets[:], offs)
 
         mark_pools = [tile([P, T], F32, "mark_pool%d" % c) for c in range(2)]
-        for c, src in enumerate((xmark, ymark)):
-            nc.sync.dma_start(mark_pools[c][P - 1 : P, :], src[0:1, :])
+        nc.sync.dma_start(mark_pools[0][P - 1 : P, :], xmark[0:1, :])
         nc.vector.memset(mark_pools[0][0 : P - 1, :].bitcast(I32), 0)
-        nc.vector.memset(mark_pools[1][0 : P - 1, :].bitcast(I32), 0)
-        q_raw = [tile([P, 4, Q], F32, "q_raw%d" % c) for c in range(2)]
-        nc.sync.dma_start(q_raw[0][:], query.rearrange("(p j) w -> p j w", j=4))
-        nc.sync.dma_start(q_raw[1][:], query2.rearrange("(p j) w -> p j w", j=4))
-        kw_pool = tile([P, T], U16, "kw_pool")
-        nc.sync.dma_start(kw_pool[:].bitcast(I32), keys_words[0].bitcast(I32))
         ks_pool = tile([P, T], U8, "ks_pool")
         for quad in range(4):
             rows = keys_scales[0, 4 * quad : 4 * quad + 4, :].bitcast(I32)
-            nc.sync.dma_start(
+            queue = nc.sync if quad < 2 else nc.gpsimd
+            queue.dma_start(
                 ks_pool[32 * quad : 32 * quad + 32, :].bitcast(I32), rows.unsqueeze(0).to_broadcast([8, 4, T // 4])
             )
+        kw_pool = tile([P, T], U16, "kw_pool")
+        nc.sync.dma_start(kw_pool[:].bitcast(I32), keys_words[0].bitcast(I32))
+        q_raw = [tile([P, 4, Q], F32, "q_raw%d" % c) for c in range(2)]
+        nc.sync.dma_start(q_raw[0][:], query.rearrange("(p j) w -> p j w", j=4))
+        nc.sync.dma_start(q_raw[1][:], query2.rearrange("(p j) w -> p j w", j=4))
+        nc.sync.dma_start(mark_pools[1][P - 1 : P, :], ymark[0:1, :])
         vals_dealt = vals.rearrange("(p t) c -> p t c", t=4)
         v_pools = [tile([P, T], F32, "v_pool%d" % t) for t in range(4)]
         nc.sync.dma_start(v_pools[0][:], vals_dealt[:, 0, :])
         lam_c = tile([P, 2], F32, "lam_c")
-        mem_c = tile([P, 2], F32, "mem_c")
         os_c = tile([P, 4], F32, "os_c")
         with nc.allow_non_contiguous_dma(reason="one value a partition"):
             nc.sync.dma_start(lam_c[:], lam.rearrange("(c p) o -> p (c o)", p=P))
-            nc.sync.dma_start(mem_c[:], memq.rearrange("o (c p) -> p (o c)", p=P))
         nc.sync.dma_start(os_c[:], slot_scale.rearrange("o (p r) -> p (o r)", r=4))
         for t in range(1, 4):
             nc.sync.dma_start(v_pools[t][:], vals_dealt[:, t, :])
+        mem_row = tile([P, Q], F32, "mem_row")
+        nc.sync.dma_start(mem_row[:], memq[0].partition_broadcast(P))
 
         ident = tile([P, P], F32, "ident")
         make_identity(nc, ident[:])
+        nc.gpsimd.memset(mark_pools[1][0 : P - 1, :].bitcast(I32), 0)
         y_prev = tile([P, 4, Q], F32, "y_prev")
         nc.gpsimd.memset(y_prev[:, :, 0:1], 0.0)
 
-        q_codes = tile([P, 2 * Q], U32, "q_codes")
-        q_scales = tile([P, 2 * Q], U8, "q_scales")
-        q_bf = [tile([P, Q, 4], BF16, "q_bf%d" % c) for c in range(2)]
+        kw = tile([P, I], U16, "kw")
+        ks = tile([P, I], U8, "ks")
+        sq = [tile([P, 2, Q], F32, "sq%d" % j) for j in range(4)]
         for c in range(2):
+            q_bf = tile([P, Q, 4], BF16, "q_bf%d" % c)
             nc.scalar.copy(
-                q_bf[c][:].rearrange("p (c i) t -> p c t i", i=4), q_raw[c][:].rearrange("p t (c i) -> p c t i", i=4)
+                q_bf[:].rearrange("p (c i) t -> p c t i", i=4), q_raw[c][:].rearrange("p t (c i) -> p c t i", i=4)
             )
-
-        marks = []
-        for c in range(2):
-            picked = tile([P, I], F32, "mark_picked%d" % c)
+            picked = tile([P, I], F32, "mark_picked%d" % c, tag="q_bf0" if c else None)
             nc.vector.tensor_copy(picked[:], mark_pools[c][:].indirect(offsets[:]))
             turned = bank(6 + c, "marks_turned%d" % c)
             for j in range(4):
                 nc.tensor.transpose(turned[:, P * j : P * (j + 1)], picked[:, P * j : P * (j + 1)], ident[:])
-            mk = tile([P, 4], F32, "marks%d" % c)
-            nc.scalar.copy(mk[:], turned[:, P - 1 :: P])
-            marks.append(mk)
-
-        scores = []
-        for h in range(2):
-            half = offsets[:, 16 * h : 16 * h + 16]
-            kw = tile([P, 256], U16, "kw%d" % h, tag="q_bf0" if h else None)
-            ks = tile([P, 256], U8, "ks%d" % h, tag="q_bf1" if h else None)
-            nc.vector.tensor_copy(kw[:], kw_pool[:].indirect(half))
-            nc.vector.tensor_copy(ks[:], ks_pool[:].indirect(half))
-            if h == 0:
-                for c in range(2):
-                    nc.vector.quantize_mx(
-                        out=q_codes[:, Q * c : Q * (c + 1)].bitcast(FP8X4),
-                        scales=q_scales[:, Q * c : Q * (c + 1)],
-                        in_=q_bf[c][:].rearrange("p q t -> p (q t)"),
+            marks = tile([P, 4], F32, "marks%d" % c)
+            nc.scalar.copy(marks[:], turned[:, P - 1 :: P])
+            if c == 0:
+                nc.vector.tensor_copy(ks[:], ks_pool[:].indirect(offsets[:]))
+                nc.vector.tensor_copy(kw[:], kw_pool[:].indirect(offsets[:]))
+            q_codes = tile([P, Q], U32, "q_codes%d" % c)
+            q_scales = tile([P, Q], U8, "q_scales%d" % c)
+            nc.vector.quantize_mx(out=q_codes[:].bitcast(FP8X4), scales=q_scales[:], in_=q_bf[:].rearrange("p q t -> p (q t)"))
+            for pair in range(2):
+                score = bank(2 * c + pair, "score%d%d" % (c, pair))
+                for jj in range(2):
+                    cols = slice(P * (2 * pair + jj), P * (2 * pair + jj + 1))
+                    nc.tensor.matmul_mx(
+                        out=score[:, Q * jj : Q * (jj + 1)], lhsT=kw[:, cols].bitcast(FP4X4), lhsT_scale=ks[:, cols],
+                        rhs=q_codes[:].bitcast(FP8X4), rhs_scale=q_scales[:], start=True, stop=True,
                     )
-            for jj in range(2):
-                cols = slice(P * jj, P * (jj + 1))
-                score = bank(2 * h + jj, "score%d%d" % (h, jj))
-                nc.tensor.matmul_mx(
-                    out=score[:], lhsT=kw[:, cols].bitcast(FP4X4), lhsT_scale=ks[:, cols],
-                    rhs=q_codes[:].bitcast(FP8X4), rhs_scale=q_scales[:], start=True, stop=True,
-                )
-                scores.append(score)
+                for jj in range(2):
+                    j = 2 * pair + jj
+                    nc.scalar.activation(
+                        sq[j][:, c, :], score[:, Q * jj : Q * (jj + 1)], ACT.Square, bias=marks[:, j : j + 1], scale=-1.0
+                    )
 
         neg_lam = tile([P, 2], F32, "neg_lam")
         nc.gpsimd.tensor_scalar(neg_lam[:], lam_c[:], -1.0, 0.0, ALU.mult, ALU.add)
 
         dist = [bank(4 + qt, "dist%d" % qt) for qt in range(2)]
         for j in range(4):
-            score = scores[j]
-            sq = tile([P, 2, Q], F32, "sq%d" % j)
-            for c in range(2):
-                nc.scalar.activation(
-                    sq[:, c, :], score[:, Q * c : Q * (c + 1)], ACT.Square, bias=marks[c][:, j : j + 1], scale=-1.0
-                )
             for qt in range(2):
                 for c in range(2):
                     nc.tensor.matmul(
-                        dist[qt][:, P * j : P * (j + 1)], sq[:, c, P * qt : P * (qt + 1)], ident[:],
+                        dist[qt][:, P * j : P * (j + 1)], sq[j][:, c, P * qt : P * (qt + 1)], ident[:],
                         start=(c == 0), stop=(c == 1), is_transpose=True,
                     )
 
-        p = tile([P, 8, 2, G], F32, "p")
+        p = tile([P, 4, 2, G, 2], F32, "p")
         z = tile([P, 2], F32, "z")
         for qt in range(2):
             nc.scalar.activation(
-                p[:, :, qt, :], dist[qt][:].rearrange("p (g j) -> p j g", j=8), ACT.Exp,
+                p[:, :, qt], dist[qt][:].rearrange("p (g e r) -> p r g e", e=2, r=4), ACT.Exp,
                 scale=neg_lam[:, qt : qt + 1], accum_out=z[:, qt : qt + 1],
             )
-        rz = tile([P, 2], F32, "rz")
-        rz_root = tile([P, 2], F32, "rz_root")
-        nc.scalar.activation(rz_root[:], z[:], ACT.Abs_reciprocal_sqrt)
-        nc.scalar.activation(rz[:], rz_root[:], ACT.Square)
 
-        v_mx = []
-        for t in range(4):
-            v_picked = tile([P, I], BF16, "v_picked%d" % t)
-            nc.vector.tensor_copy(v_picked[:], v_pools[t][:].indirect(offsets[:]))
-            words = v_picked[:].bitcast(F32)
-            v_turned = bank(6 + t % 2, "v_turned%d" % t)
-            for u in range(2):
-                nc.tensor.transpose(v_turned[:, P * u : P * (u + 1)], words[:, u::2], ident[:])
-            v_bf = tile([P, I], BF16, "v_bf%d" % t, tag=("marks1", "neg_lam", None, None)[t])
+        def gather_values(t):
+            picked = tile([P, I], BF16, "v_picked%d" % t, tag=None if t else "q_bf1")
+            nc.vector.tensor_copy(picked[:], v_pools[t][:].indirect(offsets[:]))
+            return picked
+
+        def quantize_values(planes, b, tag):
+            n = len(planes)
+            name = "v%d" % b
+            turned = bank(b, name + "_turned")
+            for k, picked in enumerate(planes):
+                words = picked[:].bitcast(F32)
+                for u in range(2):
+                    c0 = P * (2 * k + u)
+                    nc.tensor.transpose(turned[:, c0 : c0 + P], words[:, u::2], ident[:])
+            v_bf = tile([P, n * I], BF16, name + "_bf", tag=tag)
             nc.scalar.copy(
-                v_bf[:].bitcast(F32).rearrange("p (e u) -> p e u", u=2),
-                v_turned[:, 0 : 2 * P].rearrange("p (u e) -> p e u", u=2),
+                v_bf[:].bitcast(F32).rearrange("p (k e u) -> p k e u", k=n, u=2),
+                turned[:, 0 : 2 * P * n].rearrange("p (k u e) -> p k e u", k=n, u=2),
             )
-            v_codes = tile([P, P], U32, "v_codes%d" % t)
-            v_scales = tile([P, P], U8, "v_scales%d" % t)
-            nc.vector.quantize_mx(out=v_codes[:].bitcast(FP8X4), scales=v_scales[:], in_=v_bf[:])
-            v_mx.append((v_codes, v_scales))
+            codes = tile([P, n * P], U32, name + "_codes")
+            scales = tile([P, n * P], U8, name + "_scales")
+            nc.vector.quantize_mx(out=codes[:].bitcast(FP8X4), scales=scales[:], in_=v_bf[:])
+            return [(codes[:, P * k : P * (k + 1)], scales[:, P * k : P * (k + 1)]) for k in range(n)]
 
+        v_picked = [gather_values(t) for t in range(3)]
+        v_mx = quantize_values(v_picked[0:1], 6, "marks1")
+
+        rz = tile([P, 2], F32, "rz", tag="v_pool2")
+        rz2 = tile([P, 2], F32, "rz2")
+        nc.vector.reciprocal(rz[:], z[:])
+        nc.vector.tensor_tensor(rz2[:], rz[:], rz[:], ALU.mult)
+        p2 = tile([P, 2, 4, P], F32, "p2")
+
+        def square_p(qt):
+            p_qt = p[:, :, qt].rearrange("p r g e -> p r (g e)")
+            nc.vector.scalar_tensor_tensor(p2[:, qt], p_qt, rz2[:, qt : qt + 1], p_qt, ALU.mult, ALU.mult)
+
+        square_p(0)
         pg_turned = bank(0, "pg_turned")
         for j in range(8):
             nc.tensor.matmul(
-                pg_turned[:, 0:P], p[:, j].rearrange("p t g -> p (t g)"), ident[:],
+                pg_turned[:, 0:P], p[:, j // 2, :, :, j % 2].rearrange("p t g -> p (t g)"), ident[:],
                 start=(j == 0), stop=(j == 7), is_transpose=True,
             )
-        pg_t = tile([P, P], F32, "pg_t", tag="v_pool1")
+        pg_t = tile([P, P], F32, "pg_t")
         nc.vector.tensor_copy(pg_t[:], pg_turned[:, 0:P])
         pg = bank(1, "pg")
         nc.tensor.transpose(pg[:, 0:P], pg_t[:], ident[:])
+        square_p(1)
+        p2_turned = [bank(2 + pair, "p2_turned%d" % pair) for pair in range(2)]
+        for qt in range(2):
+            for r in range(4):
+                c0 = Q * (r % 2) + P * qt
+                nc.tensor.transpose(p2_turned[r // 2][:, c0 : c0 + P], p2[:, qt, r, :], ident[:])
 
         inv_rt = tile([P, 2, G], F32, "inv_rt")
         inv_pg = tile([P, 2, G], F32, "inv_pg")
-        rt = tile([P, 2, G], F32, "rt", tag="v_pool2")
+        rt = tile([P, 2, G], F32, "rt")
         rt_sum = tile([P, 2], F32, "rt_sum")
         for qt in range(2):
             nc.scalar.activation(
@@ -190,40 +200,37 @@ def tile_attend_maplace_pagewinners_rowchanges_pl_kernel(
                 accum_out=rt_sum[:, qt : qt + 1],
             )
         nc.vector.reciprocal(inv_sum[:], rt_sum[:])
-        p_dealt = p[:].rearrange("p (e r) t g -> p t r g e", r=4)
-        w_mx = []
+        k_turned = [bank(4 + qt, "k_turned%d" % qt) for qt in range(2)]
         for qt in range(2):
-            k_turned = bank(4 + qt, "k_turned%d" % qt)
             nc.vector.scalar_tensor_tensor(
                 k_twice[:, qt], inv_pg[:, qt, :].unsqueeze(2).to_broadcast([P, G, 2]), inv_sum[:, qt : qt + 1],
                 inv_rt[:, qt, :].unsqueeze(2).to_broadcast([P, G, 2]), ALU.mult, ALU.mult,
             )
-            nc.tensor.transpose(k_turned[:, 0:P], k_twice[:, qt].rearrange("p g e -> p (g e)"), ident[:])
-            p2 = tile([P, 4, G, 2], F32, "p2_%d" % qt)
-            nc.scalar.activation(p2[:], p_dealt[:, qt], ACT.Square, scale=rz[:, qt : qt + 1])
-            p2_os = tile([P, 4, P], F32, "p2_os%d" % qt)
-            p2_turned = bank(2 + qt, "p2_turned%d" % qt)
-            for r in range(4):
-                nc.tensor.transpose(p2_turned[:, P * r : P * (r + 1)], p2[:, r].rearrange("p g e -> p (g e)"), ident[:])
-            for r in range(4):
-                nc.scalar.activation(p2_os[:, r, :], p2_turned[:, P * r : P * (r + 1)], ACT.Copy, scale=os_c[:, r : r + 1])
-            w_bf = tile([P, P, 4], BF16, "w_bf%d" % qt, tag="p2_os0" if qt else "v_pool3")
+            nc.tensor.transpose(k_turned[qt][:, 0:P], k_twice[:, qt].rearrange("p g e -> p (g e)"), ident[:])
+
+        p2_os = tile([P, 4, Q], F32, "p2_os", tag="pg_t")
+        for r in range(4):
+            c0 = Q * (r % 2)
+            nc.scalar.activation(p2_os[:, r, :], p2_turned[r // 2][:, c0 : c0 + Q], ACT.Copy, scale=os_c[:, r : r + 1])
+
+        v_picked.append(gather_values(3))
+        v_mx = v_mx + quantize_values(v_picked[1:3], 0, None)
+        v_mx = v_mx + quantize_values(v_picked[3:4], 7, None)
+
+        w_mx = []
+        w_both = tile([P, 2, P, 4], BF16, "w_both", tag="v_pool3")
+        for qt in range(2):
+            w_bf = w_both[:, qt]
             nc.vector.tensor_tensor(
-                w_bf[:].rearrange("p (c i) r -> p c r i", i=4),
-                p2_os[:].rearrange("p r (c i) -> p c r i", i=4),
-                k_turned[:, 0:P].rearrange("p (c i) -> p c i", i=4).unsqueeze(2).to_broadcast([P, P // 4, 4, 4]),
+                w_bf.rearrange("p (c i) r -> p c r i", i=4),
+                p2_os[:, :, P * qt : P * (qt + 1)].rearrange("p r (c i) -> p c r i", i=4),
+                k_turned[qt][:, 0:P].rearrange("p (c i) -> p c i", i=4).unsqueeze(2).to_broadcast([P, P // 4, 4, 4]),
                 ALU.mult,
             )
             w_codes = tile([P, P], U32, "w_codes%d" % qt)
             w_scales = tile([P, P], U8, "w_scales%d" % qt)
-            nc.vector.quantize_mx(out=w_codes[:].bitcast(FP8X4), scales=w_scales[:], in_=w_bf[:].rearrange("p q r -> p (q r)"))
+            nc.vector.quantize_mx(out=w_codes[:].bitcast(FP8X4), scales=w_scales[:], in_=w_bf.rearrange("p q r -> p (q r)"))
             w_mx.append((w_codes, w_scales))
-
-        mem_turned = bank(0, "mem_turned")
-        for qt in range(2):
-            nc.tensor.transpose(mem_turned[:, P * qt : P * (qt + 1)], mem_c[:, qt : qt + 1].to_broadcast([P, P]), ident[:])
-        mem_row = tile([P, Q], F32, "mem_row")
-        nc.scalar.copy(mem_row[:], mem_turned[:, 0:Q])
 
         out_dealt = out_0.rearrange("(p t) q -> p t q", t=4)
         y_codes = tile([P, Q], U32, "y_codes")
@@ -236,7 +243,7 @@ def tile_attend_maplace_pagewinners_rowchanges_pl_kernel(
             for t in range(4):
                 v_codes, v_scales = v_mx[t]
                 nc.tensor.matmul_mx(
-                    out=o[:, P * t : P * (t + 1)], lhsT=v_codes[:].bitcast(FP8X4), lhsT_scale=v_scales[:],
+                    out=o[:, P * t : P * (t + 1)], lhsT=v_codes.bitcast(FP8X4), lhsT_scale=v_scales,
                     rhs=w_codes[:].bitcast(FP8X4), rhs_scale=w_scales[:], start=True, stop=True,
                 )
             o3 = o[:].rearrange("p (t q) -> p t q", t=4)

@@ -44,8 +44,7 @@ def tile_attend_maplace_pagewinners_rowchanges_pl_kernel(
         ks_pool = tile([P, T], U8, "ks_pool")
         for quad in range(4):
             rows = keys_scales[0, 4 * quad : 4 * quad + 4, :].bitcast(I32)
-            queue = nc.sync if quad < 2 else nc.gpsimd
-            queue.dma_start(
+            nc.sync.dma_start(
                 ks_pool[32 * quad : 32 * quad + 32, :].bitcast(I32), rows.unsqueeze(0).to_broadcast([8, 4, T // 4])
             )
         kw_pool = tile([P, T], U16, "kw_pool")
@@ -133,8 +132,7 @@ def tile_attend_maplace_pagewinners_rowchanges_pl_kernel(
             nc.vector.tensor_copy(picked[:], v_pools[t][:].indirect(offsets[:]))
             return picked
 
-        def quantize_values(planes, b, tag):
-            n = len(planes)
+        def turn_values(planes, b, tag):
             name = "v%d" % b
             turned = bank(b, name + "_turned")
             for k, picked in enumerate(planes):
@@ -142,23 +140,30 @@ def tile_attend_maplace_pagewinners_rowchanges_pl_kernel(
                 for u in range(2):
                     c0 = P * (2 * k + u)
                     nc.tensor.transpose(turned[:, c0 : c0 + P], words[:, u::2], ident[:])
-            v_bf = tile([P, n * I], BF16, name + "_bf", tag=tag)
+            v_bf = tile([P, 2 * I], BF16, name + "_bf", tag=tag)
             nc.scalar.copy(
-                v_bf[:].bitcast(F32).rearrange("p (k e u) -> p k e u", k=n, u=2),
-                turned[:, 0 : 2 * P * n].rearrange("p (k u e) -> p k e u", k=n, u=2),
+                v_bf[:].bitcast(F32).rearrange("p (k e u) -> p k e u", k=2, u=2),
+                turned[:].rearrange("p (k u e) -> p k e u", k=2, u=2),
             )
-            codes = tile([P, n * P], U32, name + "_codes")
-            scales = tile([P, n * P], U8, name + "_scales")
+            return v_bf
+
+        def quantize_values(v_bf, name, tag):
+            codes = tile([P, 2 * P], U32, name + "_codes", tag=tag)
+            scales = tile([P, 2 * P], U8, name + "_scales")
             nc.vector.quantize_mx(out=codes[:].bitcast(FP8X4), scales=scales[:], in_=v_bf[:])
-            return [(codes[:, P * k : P * (k + 1)], scales[:, P * k : P * (k + 1)]) for k in range(n)]
+            return [(codes[:, P * k : P * (k + 1)], scales[:, P * k : P * (k + 1)]) for k in range(2)]
 
         v_picked = [gather_values(t) for t in range(3)]
-        v_mx = quantize_values(v_picked[0:1], 6, "marks1")
 
-        rz = tile([P, 2], F32, "rz", tag="v_pool2")
+        z_root = tile([P, 2], F32, "z_root")
+        rz = tile([P, 2], F32, "rz")
+        nc.scalar.activation(z_root[:], z[:], ACT.Abs_reciprocal_sqrt)
+        nc.scalar.activation(rz[:], z_root[:], ACT.Square)
+        v_bf01 = turn_values(v_picked[0:2], 6, "z_root")
+        rz1 = tile([P, 2], F32, "rz1", tag="v_pool2")
         rz2 = tile([P, 2], F32, "rz2")
-        nc.vector.reciprocal(rz[:], z[:])
-        nc.vector.tensor_tensor(rz2[:], rz[:], rz[:], ALU.mult)
+        nc.vector.reciprocal(rz1[:], z[:])
+        nc.vector.tensor_tensor(rz2[:], rz1[:], rz1[:], ALU.mult)
         p2 = tile([P, 2, 4, P], F32, "p2")
 
         def square_p(qt):
@@ -166,6 +171,8 @@ def tile_attend_maplace_pagewinners_rowchanges_pl_kernel(
             nc.vector.scalar_tensor_tensor(p2[:, qt], p_qt, rz2[:, qt : qt + 1], p_qt, ALU.mult, ALU.mult)
 
         square_p(0)
+        square_p(1)
+
         pg_turned = bank(0, "pg_turned")
         for j in range(8):
             nc.tensor.matmul(
@@ -176,16 +183,16 @@ def tile_attend_maplace_pagewinners_rowchanges_pl_kernel(
         nc.vector.tensor_copy(pg_t[:], pg_turned[:, 0:P])
         pg = bank(1, "pg")
         nc.tensor.transpose(pg[:, 0:P], pg_t[:], ident[:])
-        square_p(1)
         p2_turned = [bank(2 + pair, "p2_turned%d" % pair) for pair in range(2)]
         for qt in range(2):
             for r in range(4):
                 c0 = Q * (r % 2) + P * qt
                 nc.tensor.transpose(p2_turned[r // 2][:, c0 : c0 + P], p2[:, qt, r, :], ident[:])
+        v_picked.append(gather_values(3))
 
         inv_rt = tile([P, 2, G], F32, "inv_rt")
         inv_pg = tile([P, 2, G], F32, "inv_pg")
-        rt = tile([P, 2, G], F32, "rt")
+        rt = tile([P, 2, G], F32, "rt", tag="v_pool3")
         rt_sum = tile([P, 2], F32, "rt_sum")
         for qt in range(2):
             nc.scalar.activation(
@@ -213,12 +220,11 @@ def tile_attend_maplace_pagewinners_rowchanges_pl_kernel(
             c0 = Q * (r % 2)
             nc.scalar.activation(p2_os[:, r, :], p2_turned[r // 2][:, c0 : c0 + Q], ACT.Copy, scale=os_c[:, r : r + 1])
 
-        v_picked.append(gather_values(3))
-        v_mx = v_mx + quantize_values(v_picked[1:3], 0, None)
-        v_mx = v_mx + quantize_values(v_picked[3:4], 7, None)
+        v_mx = quantize_values(v_bf01, "v01", "inv_pg")
+        v_mx = v_mx + quantize_values(turn_values(v_picked[2:4], 7, None), "v23", None)
 
         w_mx = []
-        w_both = tile([P, 2, P, 4], BF16, "w_both", tag="v_pool3")
+        w_both = tile([P, 2, P, 4], BF16, "w_both")
         for qt in range(2):
             w_bf = w_both[:, qt]
             nc.vector.tensor_tensor(

@@ -179,7 +179,7 @@ def tile_attend_maplace_pagewinners_rowchanges_pl_kernel(
                 pg_turned[:, 0:P], p[:, j // 2, :, :, j % 2].rearrange("p t g -> p (t g)"), ident[:],
                 start=(j == 0), stop=(j == 7), is_transpose=True,
             )
-        pg_t = tile([P, P], F32, "pg_t")
+        pg_t = tile([P, P], F32, "pg_t", tag="v_pool2")
         nc.vector.tensor_copy(pg_t[:], pg_turned[:, 0:P])
         pg = bank(1, "pg")
         nc.tensor.transpose(pg[:, 0:P], pg_t[:], ident[:])
@@ -215,7 +215,7 @@ def tile_attend_maplace_pagewinners_rowchanges_pl_kernel(
             )
             nc.tensor.transpose(k_turned[qt][:, 0:P], k_twice[:, qt].rearrange("p g e -> p (g e)"), ident[:])
 
-        p2_os = tile([P, 4, Q], F32, "p2_os", tag="pg_t")
+        p2_os = tile([P, 4, Q], F32, "p2_os", tag="v_pool2")
         for r in range(4):
             c0 = Q * (r % 2)
             nc.scalar.activation(p2_os[:, r, :], p2_turned[r // 2][:, c0 : c0 + Q], ACT.Copy, scale=os_c[:, r : r + 1])

@@ -111,12 +111,12 @@ def tile_attend_maplace_pagewinners_rowchanges_pl_kernel(
         nc.gpsimd.tensor_scalar(neg_lam[:], lam_c[:], -1.0, 0.0, ALU.mult, ALU.add)
 
         dist = [bank(4 + qt, "dist%d" % qt) for qt in range(2)]
-        for j in range(4):
-            for qt in range(2):
-                for c in range(2):
+        for c in range(2):
+            for j in range(4):
+                for qt in range(2):
                     nc.tensor.matmul(
                         dist[qt][:, P * j : P * (j + 1)], sq[j][:, c, P * qt : P * (qt + 1)], ident[:],
-                        start=(c == 0), stop=(c == 1), is_transpose=True,
+                        start=(c == 0 and j == 0), stop=(c == 1 and j == 3), is_transpose=True,
                     )
 
         p = tile([P, 4, 2, G, 2], F32, "p")
@@ -221,7 +221,7 @@ def tile_attend_maplace_pagewinners_rowchanges_pl_kernel(
             nc.scalar.activation(p2_os[:, r, :], p2_turned[r // 2][:, c0 : c0 + Q], ACT.Copy, scale=os_c[:, r : r + 1])
 
         v_mx = quantize_values(v_bf01, "v01", "inv_pg")
-        v_mx = v_mx + quantize_values(turn_values(v_picked[2:4], 7, None), "v23", None)
+        v_mx = v_mx + quantize_values(turn_values(v_picked[2:4], 0, None), "v23", None)
 
         w_mx = []
         w_both = tile([P, 2, P, 4], BF16, "w_both")

from contextlib import ExitStack

import concourse.mybir as mybir
from concourse.masks import make_identity

D, T, I, Q, E, G = 512, 2048, 512, 256, 512, 64
FLOPS = 2 * D * I * Q * 2 + 2 * I * E * Q

F32 = mybir.dt.float32
BF16 = mybir.dt.bfloat16
I32 = mybir.dt.int32
U32 = mybir.dt.uint32
U16 = mybir.dt.uint16
U8 = mybir.dt.uint8
FP8X4 = mybir.dt.float8_e4m3fn_x4
FP4X4 = mybir.dt.float4_e2m1fn_x4
ACT = mybir.ActivationFunctionType
ALU = mybir.AluOpType

P = 128
TINY = 2.0 ** -80


def tile_attend_maplace_pagewinners_rowchanges_pl_kernel(
    tc, query, query2, keys_words, keys_scales, xmark, ymark, lam, slot_scale, vals, memq, offs, out_0, out_1, out_2
):
    nc = tc.nc
    with ExitStack() as ctx:
        sb = ctx.enter_context(tc.tile_pool(name="sb", bufs=1))
        ps = ctx.enter_context(tc.psum_pool(name="ps", bufs=1))

        def bank(b, name):
            return ps.tile([P, 512], F32, name=name, tag="bank%d" % b)

        def tile(shape, dtype, name, tag=None):
            return sb.tile(shape, dtype, name=name, tag=tag or name, align_bytes=64)

        offsets = sb.tile([P, I // 16], U16, name="offsets")
        nc.sync.dma_start(offsets[:], offs)

        mark_pools = [tile([P, T], F32, "mark_pool%d" % c) for c in range(2)]
        nc.sync.dma_start(mark_pools[0][P - 1 : P, :], xmark[0:1, :])
        nc.vector.memset(mark_pools[0][0 : P - 1, :].bitcast(I32), 0)
        ks_pool = tile([P, T], U8, "ks_pool")
        for quad in range(4):
            rows = keys_scales[0, 4 * quad : 4 * quad + 4, :].bitcast(I32)
            nc.sync.dma_start(
                ks_pool[32 * quad : 32 * quad + 32, :].bitcast(I32), rows.unsqueeze(0).to_broadcast([8, 4, T // 4])
            )
        kw_pool = tile([P, T], U16, "kw_pool")
        nc.sync.dma_start(kw_pool[:].bitcast(I32), keys_words[0].bitcast(I32))
        q_raw = [tile([P, 4, Q], F32, "q_raw%d" % c) for c in range(2)]
        nc.sync.dma_start(q_raw[0][:], query.rearrange("(p j) w -> p j w", j=4))
        nc.sync.dma_start(q_raw[1][:], query2.rearrange("(p j) w -> p j w", j=4))
        nc.sync.dma_start(mark_pools[1][P - 1 : P, :], ymark[0:1, :])
        vals_dealt = vals.rearrange("(p t) c -> p t c", t=4)
        v_pools = [tile([P, T], F32, "v_pool%d" % t) for t in range(4)]
        nc.sync.dma_start(v_pools[0][:], vals_dealt[:, 0, :])
        lam_c = tile([P, 2], F32, "lam_c")
        os_c = tile([P, 4], F32, "os_c")
        with nc.allow_non_contiguous_dma(reason="one value a partition"):
            nc.sync.dma_start(lam_c[:], lam.rearrange("(c p) o -> p (c o)", p=P))
        nc.sync.dma_start(os_c[:], slot_scale.rearrange("o (p r) -> p (o r)", r=4))
        for t in range(1, 4):
            nc.sync.dma_start(v_pools[t][:], vals_dealt[:, t, :])
        mem_row = tile([P, Q], F32, "mem_row")
        nc.sync.dma_start(mem_row[:], memq[0].partition_broadcast(P))

        ident = tile([P, P], F32, "ident")
        make_identity(nc, ident[:])
        nc.gpsimd.memset(mark_pools[1][0 : P - 1, :].bitcast(I32), 0)
        y_prev = tile([P, 4, Q], F32, "y_prev")
        nc.gpsimd.memset(y_prev[:, :, 0:1], 0.0)

        kw = tile([P, I], U16, "kw")
        ks = tile([P, I], U8, "ks")
        sq = [tile([P, 2, Q], F32, "sq%d" % j) for j in range(4)]
        for c in range(2):
            q_bf = tile([P, Q, 4], BF16, "q_bf%d" % c)
            nc.scalar.copy(
                q_bf[:].rearrange("p (c i) t -> p c t i", i=4), q_raw[c][:].rearrange("p t (c i) -> p c t i", i=4)
            )
            picked = tile([P, I], F32, "mark_picked%d" % c, tag="q_bf0" if c else None)
            nc.vector.tensor_copy(picked[:], mark_pools[c][:].indirect(offsets[:]))
            turned = bank(6 + c, "marks_turned%d" % c)
            for j in range(4):
                nc.tensor.transpose(turned[:, P * j : P * (j + 1)], picked[:, P * j : P * (j + 1)], ident[:])
            marks = tile([P, 4], F32, "marks%d" % c)
            nc.scalar.copy(marks[:], turned[:, P - 1 :: P])
            if c == 0:
                nc.vector.tensor_copy(ks[:], ks_pool[:].indirect(offsets[:]))
                nc.vector.tensor_copy(kw[:], kw_pool[:].indirect(offsets[:]))
            q_codes = tile([P, Q], U32, "q_codes%d" % c)
            q_scales = tile([P, Q], U8, "q_scales%d" % c)
            nc.vector.quantize_mx(out=q_codes[:].bitcast(FP8X4), scales=q_scales[:], in_=q_bf[:].rearrange("p q t -> p (q t)"))
            for pair in range(2):
                score = bank(2 * c + pair, "score%d%d" % (c, pair))
                for jj in range(2):
                    cols = slice(P * (2 * pair + jj), P * (2 * pair + jj + 1))
                    nc.tensor.matmul_mx(
                        out=score[:, Q * jj : Q * (jj + 1)], lhsT=kw[:, cols].bitcast(FP4X4), lhsT_scale=ks[:, cols],
                        rhs=q_codes[:].bitcast(FP8X4), rhs_scale=q_scales[:], start=True, stop=True,
                    )
                for jj in range(2):
                    j = 2 * pair + jj
                    nc.scalar.activation(
                        sq[j][:, c, :], score[:, Q * jj : Q * (jj + 1)], ACT.Square, bias=marks[:, j : j + 1], scale=-1.0
                    )

        neg_lam = tile([P, 2], F32, "neg_lam")
        nc.gpsimd.tensor_scalar(neg_lam[:], lam_c[:], -1.0, 0.0, ALU.mult, ALU.add)

        dist = [bank(4 + qt, "dist%d" % qt) for qt in range(2)]
        for c in range(2):
            for j in range(4):
                for qt in range(2):
                    nc.tensor.matmul(
                        dist[qt][:, P * j : P * (j + 1)], sq[j][:, c, P * qt : P * (qt + 1)], ident[:],
                        start=(c == 0 and j == 0), stop=(c == 1 and j == 3), is_transpose=True,
                    )

        p = tile([P, 4, 2, G, 2], F32, "p")
        z = tile([P, 2], F32, "z")
        for qt in range(2):
            nc.scalar.activation(
                p[:, :, qt], dist[qt][:].rearrange("p (g e r) -> p r g e", e=2, r=4), ACT.Exp,
                scale=neg_lam[:, qt : qt + 1], accum_out=z[:, qt : qt + 1],
            )

        def gather_values(t):
            picked = tile([P, I], BF16, "v_picked%d" % t, tag=None if t else "q_bf1")
            nc.vector.tensor_copy(picked[:], v_pools[t][:].indirect(offsets[:]))
            return picked

        def turn_values(planes, b, tag):
            name = "v%d" % b
            turned = bank(b, name + "_turned")
            for k, picked in enumerate(planes):
                words = picked[:].bitcast(F32)
                for u in range(2):
                    c0 = P * (2 * k + u)
                    nc.tensor.transpose(turned[:, c0 : c0 + P], words[:, u::2], ident[:])
            v_bf = tile([P, 2 * I], BF16, name + "_bf", tag=tag)
            nc.scalar.copy(
                v_bf[:].bitcast(F32).rearrange("p (k e u) -> p k e u", k=2, u=2),
                turned[:].rearrange("p (k u e) -> p k e u", k=2, u=2),
            )
            return v_bf

        def quantize_values(v_bf, name, tag):
            codes = tile([P, 2 * P], U32, name + "_codes", tag=tag)
            scales = tile([P, 2 * P], U8, name + "_scales")
            nc.vector.quantize_mx(out=codes[:].bitcast(FP8X4), scales=scales[:], in_=v_bf[:])
            return [(codes[:, P * k : P * (k + 1)], scales[:, P * k : P * (k + 1)]) for k in range(2)]

        v_picked = [gather_values(t) for t in range(3)]

        z_root = tile([P, 2], F32, "z_root")
        rz = tile([P, 2], F32, "rz")
        nc.scalar.activation(z_root[:], z[:], ACT.Abs_reciprocal_sqrt)
        nc.scalar.activation(rz[:], z_root[:], ACT.Square)
        v_bf01 = turn_values(v_picked[0:2], 6, "z_root")
        rz1 = tile([P, 2], F32, "rz1", tag="v_pool2")
        rz2 = tile([P, 2], F32, "rz2")
        nc.vector.reciprocal(rz1[:], z[:])
        nc.vector.tensor_tensor(rz2[:], rz1[:], rz1[:], ALU.mult)
        p2 = tile([P, 2, 4, P], F32, "p2")

        def square_p(qt):
            p_qt = p[:, :, qt].rearrange("p r g e -> p r (g e)")
            nc.vector.scalar_tensor_tensor(p2[:, qt], p_qt, rz2[:, qt : qt + 1], p_qt, ALU.mult, ALU.mult)

        square_p(0)
        square_p(1)

        pg_turned = bank(0, "pg_turned")
        for j in range(8):
            nc.tensor.matmul(
                pg_turned[:, 0:P], p[:, j // 2, :, :, j % 2].rearrange("p t g -> p (t g)"), ident[:],
                start=(j == 0), stop=(j == 7), is_transpose=True,
            )
        pg_t = tile([P, P], F32, "pg_t", tag="v_pool2")
        nc.vector.tensor_copy(pg_t[:], pg_turned[:, 0:P])
        pg = bank(1, "pg")
        nc.tensor.transpose(pg[:, 0:P], pg_t[:], ident[:])
        p2_turned = [bank(2 + pair, "p2_turned%d" % pair) for pair in range(2)]
        for qt in range(2):
            for r in range(4):
                c0 = Q * (r % 2) + P * qt
                nc.tensor.transpose(p2_turned[r // 2][:, c0 : c0 + P], p2[:, qt, r, :], ident[:])
        v_picked.append(gather_values(3))

        inv_rt = tile([P, 2, G], F32, "inv_rt")
        inv_pg = tile([P, 2, G], F32, "inv_pg")
        rt = tile([P, 2, G], F32, "rt", tag="v_pool3")
        rt_sum = tile([P, 2], F32, "rt_sum")
        for qt in range(2):
            nc.scalar.activation(
                inv_rt[:, qt, :], pg[:, G * qt : G * (qt + 1)], ACT.Abs_reciprocal_sqrt, bias=TINY, scale=rz[:, qt : qt + 1]
            )
        nc.scalar.activation(inv_pg[:], inv_rt[:], ACT.Square)
        inv_sum = tile([P, 2], F32, "inv_sum")
        k_twice = tile([P, 2, G, 2], F32, "k_twice")
        for qt in range(2):
            nc.vector.scalar_tensor_tensor(
                rt[:, qt, :], pg[:, G * qt : G * (qt + 1)], rz[:, qt : qt + 1], inv_rt[:, qt, :], ALU.mult, ALU.mult,
                accum_out=rt_sum[:, qt : qt + 1],
            )
        nc.vector.reciprocal(inv_sum[:], rt_sum[:])
        k_turned = [bank(4 + qt, "k_turned%d" % qt) for qt in range(2)]
        for qt in range(2):
            nc.vector.scalar_tensor_tensor(
                k_twice[:, qt], inv_pg[:, qt, :].unsqueeze(2).to_broadcast([P, G, 2]), inv_sum[:, qt : qt + 1],
                inv_rt[:, qt, :].unsqueeze(2).to_broadcast([P, G, 2]), ALU.mult, ALU.mult,
            )
            nc.tensor.transpose(k_turned[qt][:, 0:P], k_twice[:, qt].rearrange("p g e -> p (g e)"), ident[:])

        p2_os = tile([P, 4, Q], F32, "p2_os", tag="v_pool2")
        for r in range(4):
            c0 = Q * (r % 2)
            nc.scalar.activation(p2_os[:, r, :], p2_turned[r // 2][:, c0 : c0 + Q], ACT.Copy, scale=os_c[:, r : r + 1])

        v_mx = quantize_values(v_bf01, "v01", "inv_pg")
        v_mx = v_mx + quantize_values(turn_values(v_picked[2:4], 0, None), "v23", None)

        w_mx = []
        w_both = tile([P, 2, P, 4], BF16, "w_both")
        for qt in range(2):
            w_bf = w_both[:, qt]
            nc.vector.tensor_tensor(
                w_bf.rearrange("p (c i) r -> p c r i", i=4),
                p2_os[:, :, P * qt : P * (qt + 1)].rearrange("p r (c i) -> p c r i", i=4),
                k_turned[qt][:, 0:P].rearrange("p (c i) -> p c i", i=4).unsqueeze(2).to_broadcast([P, P // 4, 4, 4]),
                ALU.mult,
            )
            w_codes = tile([P, P], U32, "w_codes%d" % qt)
            w_scales = tile([P, P], U8, "w_scales%d" % qt)
            nc.vector.quantize_mx(out=w_codes[:].bitcast(FP8X4), scales=w_scales[:], in_=w_bf.rearrange("p q r -> p (q r)"))
            w_mx.append((w_codes, w_scales))

        out_dealt = out_0.rearrange("(p t) q -> p t q", t=4)
        y_codes = tile([P, Q], U32, "y_codes")
        y_scales = tile([P, Q], U8, "y_scales")
        words_out = out_1[0].rearrange("p c r -> p (c r)").bitcast(I32)
        for qt in range(2):
            w_codes, w_scales = w_mx[qt]
            cols = slice(P * qt, P * (qt + 1))
            o = bank(qt, "o%d" % qt)
            for t in range(4):
                v_codes, v_scales = v_mx[t]
                nc.tensor.matmul_mx(
                    out=o[:, P * t : P * (t + 1)], lhsT=v_codes.bitcast(FP8X4), lhsT_scale=v_scales,
                    rhs=w_codes[:].bitcast(FP8X4), rhs_scale=w_scales[:], start=True, stop=True,
                )
            o3 = o[:].rearrange("p (t q) -> p t q", t=4)
            n = P - qt
            nxt = slice(P * qt + 1, P * qt + 1 + n)
            nc.vector.tensor_tensor(
                y_prev[:, :, nxt], o3[:, :, 0:n], mem_row[:, nxt].unsqueeze(1).to_broadcast([P, 4, n]), ALU.mult
            )
            y = tile([P, 4, P], F32, "y%d" % qt)
            nc.vector.tensor_tensor(y[:], o3, y_prev[:, :, cols], ALU.subtract)
            nc.sync.dma_start(out_dealt[:, :, cols], y[:])
            y_bf = tile([P, P, 4], BF16, "y_bf%d" % qt)
            nc.scalar.copy(y_bf[:].rearrange("p (c i) t -> p c t i", i=4), y[:].rearrange("p t (c i) -> p c t i", i=4))
            nc.vector.quantize_mx(
                out=y_codes[:, cols].bitcast(FP8X4), scales=y_scales[:, cols], in_=y_bf[:].rearrange("p q t -> p (q t)")
            )
            nc.sync.dma_start(words_out[:, cols], y_codes[:, cols].bitcast(I32))
        for quad in range(4):
            queue = nc.scalar if quad % 2 else nc.sync
            queue.dma_start(
                out_2[0, 4 * quad : 4 * quad + 4, :].bitcast(I32), y_scales[32 * quad : 32 * quad + 4, :].bitcast(I32)
            )
